import numpy as np
import ml_dtypes


def mxq(x, axis, fmt="e4m3"):
    dtype, down = {"e4m3": (ml_dtypes.float8_e4m3fn, 7), "e5m2": (ml_dtypes.float8_e5m2, 14)}[fmt]
    v = np.moveaxis(np.asarray(x, np.float32).astype(ml_dtypes.bfloat16).astype(np.float64), axis, -1)
    blocks = v.reshape(v.shape[:-1] + (-1, 32))
    amax = np.abs(blocks).max(-1, keepdims=True)
    byte = np.maximum(np.where(amax > 0, np.frexp(amax)[1] - 1 + 127, 0) - down, 1)
    scale = np.exp2(byte - 127.0)
    codes = (blocks / scale).astype(np.float32).astype(dtype).astype(np.float64)
    return np.moveaxis((codes * scale).reshape(v.shape), -1, axis)


WIDE = False


def mx_kscale(k):
    if not WIDE:
        return np.ones(k)
    levels = np.array([10, -10, 5, -5, 0])
    if k % 512:
        return np.exp2(np.random.permutation(np.resize(levels, k // 32))).repeat(32)
    a = np.empty((k // 512, 16))
    for p in range(k // 512):
        a[p, :8] = np.random.permutation(np.resize(levels, 8))
        for g in range(8):
            far = levels[np.abs(levels - a[p, g]) >= 10]
            a[p, g + 8] = far[np.random.randint(len(far))]
    return np.exp2(a.ravel()).repeat(32)


def f64(x):
    return np.asarray(x).astype(np.float64)


def striped(idx):
    return np.tile(idx.reshape(-1, 16).T, (8, 1)).astype(np.uint16)


def unstriped(offs):
    return offs[:16].T.reshape(-1).astype(np.int64)


def silu(v):
    return v / (1.0 + np.exp(-np.maximum(v, -700.0)))


K, T, E, C, H, N = 512, 2048, 8, 128, 1024, 128


def by_expert(wq, xq):
    return np.concatenate([wq[e].T @ xq[:, e * C:(e + 1) * C] for e in range(E)], axis=1)


def setup_inputs():
    n = np.random.standard_normal
    s = mx_kscale(K)[:, None]
    u = mx_kscale(H)
    return {
        "xT": (n((K, T)) * s).astype(np.float32),
        "w1": (n((E, K, H)) / np.sqrt(K) / s[None] * u[None, None, :]).astype(np.float32),
        "w2": (n((E, H, N)) / np.sqrt(H) / u[None, :, None]).astype(np.float32),
        "gate": np.tile(np.random.uniform(0.2, 1.0, E * C), (N, 1)).astype(np.float32),
        "offs": striped(np.random.permutation(T)[:E * C]),
    }


def reference(xT, w1, w2, gate, offs):
    idx = unstriped(offs)
    xq = mxq(f64(xT)[:, idx], 0, "e4m3")
    h = silu(by_expert(mxq(f64(w1), 1, "e4m3"), xq))
    y = by_expert(mxq(f64(w2), 1, "e4m3"), mxq(h, 0, "e4m3"))
    out = np.zeros((N, T))
    out[:, idx] = f64(gate) * y
    return out

@@ -1,0 +1,259 @@
+from contextlib import ExitStack
+
+import concourse.mybir as mybir
+
+K, T, E, C, H, N = 512, 2048, 8, 128, 1024, 128
+FLOPS = 2 * E * C * (K * H + H * N)
+
+F32 = mybir.dt.float32
+BF16 = mybir.dt.bfloat16
+U32 = mybir.dt.uint32
+U16 = mybir.dt.uint16
+U8 = mybir.dt.uint8
+FP8X4 = mybir.dt.float8_e4m3fn_x4
+SILU = mybir.ActivationFunctionType.Silu
+MULT = mybir.AluOpType.mult
+
+P = 128
+PACK = 4
+PASS = P * PACK
+G = H // PASS
+PAIR = 2 * C
+HALF = T // 2
+MV = 70
+MV_TAIL = {(6, 0): 64, (6, 1): 64, (7, 0): 48, (7, 1): 48}
+
+
+def tile_routed_moe_kernel(tc, xT, w1, w2, gate, offs, out):
+    nc = tc.nc
+    with ExitStack() as ctx:
+        keep = ctx.enter_context(tc.tile_pool(name="keep", bufs=1))
+        raw = ctx.enter_context(tc.tile_pool(name="raw", bufs=1))
+        w2raw = ctx.enter_context(tc.tile_pool(name="w2raw", bufs=E))
+        work4 = ctx.enter_context(tc.tile_pool(name="work4", bufs=4))
+        work3 = ctx.enter_context(tc.tile_pool(name="work3", bufs=3))
+        psum_a = ctx.enter_context(tc.psum_pool(name="psum_a", bufs=4))
+        psum_y = ctx.enter_context(tc.psum_pool(name="psum_y", bufs=2))
+
+        offs_t = keep.tile([P, E * C // 16], U16, name="offs_t")
+        nc.sync.dma_start(offs_t[:], offs)
+
+        warm_in = keep.tile([P, 1], F32, name="warm_in")
+        warm_out = keep.tile([P, 1], F32, name="warm_out")
+        nc.vector.memset(warm_in[:], 0.0)
+        nc.scalar.activation(warm_out[:], warm_in[:], SILU)
+
+        win = keep.tile([P, T], F32, name="win")
+        nc.vector.memset(win[:], 0.0)
+
+        xv = xT.rearrange("(p j) n -> p j n", j=PACK)
+        xr, w1r, w2r = {}, {}, {}
+        gate_t = {}
+
+        def load_gate(q0, q1):
+            t_ = keep.tile([P, (q1 - q0) * PAIR], F32, name="gate%d" % q0)
+            nc.sync.dma_start(out=t_[:], in_=gate[:, q0 * PAIR : q1 * PAIR])
+            for q in range(q0, q1):
+                gate_t[q] = t_[:, (q - q0) * PAIR : (q - q0 + 1) * PAIR]
+
+        def load_x(u, hf, slot):
+            t_ = raw.tile([P, 2, HALF], F32, tag="slot%d" % slot, name="xr")
+            nc.sync.dma_start(out=t_[:], in_=xv[:, 2 * u : 2 * u + 2, hf * HALF : (hf + 1) * HALF])
+            xr[(u, hf)] = t_
+
+        def load_w1(e, slot):
+            t_ = raw.tile([P, PACK, H], F32, tag="slot%d" % slot, name="w1r")
+            nc.sync.dma_start(out=t_[:], in_=w1[e].rearrange("(p j) i -> p j i", j=PACK))
+            for g in range(G):
+                w1r[(e, g)] = t_[:, :, g * PASS : (g + 1) * PASS]
+
+        def load_w1_half(e, g, slot):
+            t_ = raw.tile([P, PACK, PASS], F32, tag="slot%d" % slot, name="w1rh")
+            nc.sync.dma_start(
+                out=t_[:], in_=w1[e][:, g * PASS : (g + 1) * PASS].rearrange("(p j) i -> p j i", j=PACK)
+            )
+            w1r[(e, g)] = t_[:]
+
+        def load_w2(e):
+            t_ = w2raw.tile([P, G, PACK, N], F32, name="w2r")
+            nc.sync.dma_start(out=t_[:], in_=w2[e].rearrange("(g p j) n -> p g j n", g=G, j=PACK))
+            w2r[e] = t_
+
+        xb = [keep.tile([P, 2 * T], BF16, name="xb%d" % u) for u in range(2)]
+        xg = keep.tile([P, E * C * PACK], BF16, name="xg", align_bytes=64)
+        xg_words = xg[:].bitcast(U32).rearrange("p (s u) -> p s u", u=2)
+        xc = keep.tile([P, E * C], U32, name="xc", align_bytes=64)
+        xs = keep.tile([P, E * C], U8, name="xs", align_bytes=64)
+
+        def cast_x(u, hf, eng):
+            dst = xb[u][:, hf * 2 * HALF : (hf + 1) * 2 * HALF].rearrange("p (n e) -> p n e", e=2)
+            src = xr[(u, hf)][:].rearrange("p e n -> p n e")
+            if eng == "S":
+                nc.scalar.copy(out=dst, in_=src)
+            else:
+                nc.vector.tensor_copy(out=dst, in_=src)
+
+        def gather_x(u):
+            nc.vector.tensor_copy(out=xg_words[:, :, u], in_=xb[u][:].bitcast(U32).indirect(offs_t[:]))
+
+        w1g, w1c, w1s, w2g, w2c, w2s, pa, hb, hc, hs, py, ysb = {}, {}, {}, {}, {}, {}, {}, {}, {}, {}, {}, {}
+
+        def copy_w1(e, g, mv):
+            grp = work4.tile([P, PACK * PASS], BF16, name="w1g", align_bytes=64)
+            dst = grp[:].rearrange("p (t m j) -> p m j t", t=PACK, j=PACK)
+            src = w1r[(e, g)].rearrange("p j (m t) -> p m j t", t=PACK)
+            nc.vector.tensor_copy(out=dst[:, 0:mv], in_=src[:, 0:mv])
+            nc.scalar.copy(out=dst[:, mv:P], in_=src[:, mv:P])
+            w1g[(e, g)] = grp
+
+        def quant_w1(e, g):
+            c_ = work4.tile([P, PASS], U32, name="w1c", align_bytes=64)
+            s_ = work4.tile([P, PASS], U8, name="w1s", align_bytes=64)
+            nc.vector.quantize_mx(out=c_[:].bitcast(FP8X4), scales=s_[:], in_=w1g[(e, g)][:])
+            w1c[(e, g)], w1s[(e, g)] = c_, s_
+
+        def copy_w2(e, eng):
+            grp2 = work3.tile([P, G * N * PACK], BF16, name="w2g", align_bytes=64)
+            dst = grp2[:].rearrange("p (g n j) -> p g n j", g=G, j=PACK)
+            src = w2r[e][:].rearrange("p g j n -> p g n j")
+            if eng == "S":
+                nc.scalar.copy(out=dst, in_=src)
+            else:
+                nc.vector.tensor_copy(out=dst, in_=src)
+            w2g[e] = grp2
+
+        def quant_w2(e):
+            c_ = work3.tile([P, G * N], U32, name="w2c", align_bytes=64)
+            s_ = work3.tile([P, G * N], U8, name="w2s", align_bytes=64)
+            nc.vector.quantize_mx(out=c_[:].bitcast(FP8X4), scales=s_[:], in_=w2g[e][:])
+            w2c[e], w2s[e] = c_, s_
+
+        def mm1(e, g):
+            slots = slice(e * C, (e + 1) * C)
+            p_ = psum_a.tile([P, PACK, C], F32, name="pa")
+            for t in range(PACK):
+                cols = slice(t * P, (t + 1) * P)
+                nc.tensor.matmul_mx(
+                    out=p_[:, t, :],
+                    lhsT=w1c[(e, g)][:, cols].bitcast(FP8X4),
+                    lhsT_scale=w1s[(e, g)][:, cols],
+                    rhs=xc[:, slots].bitcast(FP8X4),
+                    rhs_scale=xs[:, slots],
+                    start=True,
+                    stop=True,
+                )
+            pa[(e, g)] = p_
+
+        def silu(e, g):
+            if g == 0:
+                hb[e] = work3.tile([P, G * C * PACK], BF16, name="hb", align_bytes=64)
+                hc[e] = work3.tile([P, G * C], U32, name="hc", align_bytes=64)
+                hs[e] = work3.tile([P, G * C], U8, name="hs", align_bytes=64)
+            nc.scalar.activation(
+                hb[e][:, g * C * PACK : (g + 1) * C * PACK].rearrange("p (s t) -> p s t", t=PACK),
+                pa[(e, g)][:].rearrange("p t s -> p s t"),
+                SILU,
+            )
+
+        def quant_h(e, gs):
+            a, b = gs[0], gs[-1] + 1
+            nc.vector.quantize_mx(
+                out=hc[e][:, a * C : b * C].bitcast(FP8X4),
+                scales=hs[e][:, a * C : b * C],
+                in_=hb[e][:, a * C * PACK : b * C * PACK],
+            )
+
+        def mm2(e):
+            if e % 2 == 0:
+                py[e // 2] = psum_y.tile([P, PAIR], F32, name="py")
+            half = slice((e % 2) * C, (e % 2 + 1) * C)
+            for g in range(G):
+                cols = slice(g * P, (g + 1) * P)
+                nc.tensor.matmul_mx(
+                    out=py[e // 2][:, half],
+                    lhsT=w2c[e][:, cols].bitcast(FP8X4),
+                    lhsT_scale=w2s[e][:, cols],
+                    rhs=hc[e][:, cols].bitcast(FP8X4),
+                    rhs_scale=hs[e][:, cols],
+                    start=(g == 0),
+                    stop=(g == G - 1),
+                )
+
+        def ycopy(q, slot):
+            if slot is None:
+                ysb[q] = work3.tile([P, PAIR], F32, name="ysb")
+                nc.vector.tensor_copy(out=ysb[q][:], in_=py[q][:])
+            else:
+                ysb[q] = raw.tile([P, PAIR], F32, tag="slot%d" % slot, name="ysb_s")
+                nc.scalar.copy(out=ysb[q][:], in_=py[q][:])
+
+        def scatter(q):
+            nc.vector.tensor_tensor(
+                win[:].indirect(offs_t[:, q * (PAIR // 16) : (q + 1) * (PAIR // 16)]),
+                ysb[q][:],
+                gate_t[q],
+                MULT,
+            )
+
+        load_x(0, 0, 0)
+        load_x(0, 1, 1)
+        load_x(1, 0, 2)
+        load_x(1, 1, 3)
+        load_w1(0, 4)
+        load_w2(0)
+        load_w2(1)
+        load_gate(0, 2)
+        load_w1(1, 5)
+        load_w2(2)
+        load_w1(2, 6)
+
+        cast_x(0, 0, "V")
+        cast_x(0, 1, "S")
+        gather_x(0)
+        cast_x(1, 0, "S")
+        cast_x(1, 1, "V")
+        gather_x(1)
+        nc.vector.quantize_mx(out=xc[:].bitcast(FP8X4), scales=xs[:], in_=xg[:])
+
+        load_w2(3)
+        load_w1(3, 0)
+        load_w2(4)
+        load_w1(4, 1)
+        load_w2(5)
+        load_w1(5, 2)
+        load_w1_half(6, 0, 3)
+
+        y_slot = {0: 6, 1: 1, 2: 4}
+        for e in range(E):
+            copy_w1(e, 0, MV_TAIL.get((e, 0), MV))
+            copy_w1(e, 1, MV_TAIL.get((e, 1), MV))
+            if e == 0:
+                load_w1_half(6, 1, 4)
+                load_gate(2, 3)
+            if e == 1:
+                load_w1_half(7, 0, 5)
+            if e % 2 == 0 and e > 0:
+                q = e // 2 - 1
+                ycopy(q, y_slot[q])
+                scatter(q)
+                if q == 0:
+                    load_w1_half(7, 1, 6)
+                    load_w2(6)
+                    load_w2(7)
+                    load_gate(3, 4)
+            copy_w2(e, "V" if e == 7 else "S")
+            for g in range(G):
+                quant_w1(e, g)
+                mm1(e, g)
+            quant_w2(e)
+            for g in range(G):
+                silu(e, g)
+                if e == E - 1:
+                    quant_h(e, (g,))
+            if e < E - 1:
+                quant_h(e, (0, 1))
+            mm2(e)
+        ycopy(3, None)
+        scatter(3)
+
+        nc.sync.dma_start(out=out, in_=win[:])

@@ -19,7 +19,7 @@ PACK = 4
 PASS = P * PACK
 G = H // PASS
 PAIR = 2 * C
-HALF = T // 2
+XV = 1344
 MV = 70
 MV_TAIL = {(6, 0): 64, (6, 1): 64, (7, 0): 48, (7, 1): 48}
 
@@ -56,10 +56,10 @@ def tile_routed_moe_kernel(tc, xT, w1, w2, gate, offs, out):
             for q in range(q0, q1):
                 gate_t[q] = t_[:, (q - q0) * PAIR : (q - q0 + 1) * PAIR]
 
-        def load_x(u, hf, slot):
-            t_ = raw.tile([P, 2, HALF], F32, tag="slot%d" % slot, name="xr")
-            nc.sync.dma_start(out=t_[:], in_=xv[:, 2 * u : 2 * u + 2, hf * HALF : (hf + 1) * HALF])
-            xr[(u, hf)] = t_
+        def load_x(u, slot):
+            t_ = raw.tile([P, 2, T], F32, tag="slot%d" % slot, name="xr")
+            nc.sync.dma_start(out=t_[:], in_=xv[:, 2 * u : 2 * u + 2, :])
+            xr[u] = t_
 
         def load_w1(e, slot):
             t_ = raw.tile([P, PACK, H], F32, tag="slot%d" % slot, name="w1r")
@@ -85,9 +85,9 @@ def tile_routed_moe_kernel(tc, xT, w1, w2, gate, offs, out):
         xc = keep.tile([P, E * C], U32, name="xc", align_bytes=64)
         xs = keep.tile([P, E * C], U8, name="xs", align_bytes=64)
 
-        def cast_x(u, hf, eng):
-            dst = xb[u][:, hf * 2 * HALF : (hf + 1) * 2 * HALF].rearrange("p (n e) -> p n e", e=2)
-            src = xr[(u, hf)][:].rearrange("p e n -> p n e")
+        def cast_x(u, a, b, eng):
+            dst = xb[u][:, 2 * a : 2 * b].rearrange("p (n e) -> p n e", e=2)
+            src = xr[u][:, :, a:b].rearrange("p e n -> p n e")
             if eng == "S":
                 nc.scalar.copy(out=dst, in_=src)
             else:
@@ -195,10 +195,8 @@ def tile_routed_moe_kernel(tc, xT, w1, w2, gate, offs, out):
                 MULT,
             )
 
-        load_x(0, 0, 0)
-        load_x(0, 1, 1)
-        load_x(1, 0, 2)
-        load_x(1, 1, 3)
+        load_x(0, 0)
+        load_x(1, 1)
         load_w1(0, 4)
         load_w2(0)
         load_w2(1)
@@ -207,12 +205,10 @@ def tile_routed_moe_kernel(tc, xT, w1, w2, gate, offs, out):
         load_w2(2)
         load_w1(2, 6)
 
-        cast_x(0, 0, "V")
-        cast_x(0, 1, "S")
-        gather_x(0)
-        cast_x(1, 0, "S")
-        cast_x(1, 1, "V")
-        gather_x(1)
+        for u in range(2):
+            cast_x(u, 0, XV, "V")
+            cast_x(u, XV, T, "S")
+            gather_x(u)
         nc.vector.quantize_mx(out=xc[:].bitcast(FP8X4), scales=xs[:], in_=xg[:])
 
         load_w2(3)

@@ -217,14 +217,13 @@ def tile_routed_moe_kernel(tc, xT, w1, w2, gate, offs, out):
         load_w1(4, 1)
         load_w2(5)
         load_w1(5, 2)
-        load_w1_half(6, 0, 3)
+        load_w1(6, 3)
 
-        y_slot = {0: 6, 1: 1, 2: 4}
+        y_slot = {0: 6, 1: 1, 2: 3}
         for e in range(E):
             copy_w1(e, 0, MV_TAIL.get((e, 0), MV))
             copy_w1(e, 1, MV_TAIL.get((e, 1), MV))
             if e == 0:
-                load_w1_half(6, 1, 4)
                 load_gate(2, 3)
             if e == 1:
                 load_w1_half(7, 0, 5)

@@ -20,8 +20,8 @@ PASS = P * PACK
 G = H // PASS
 PAIR = 2 * C
 XV = 1344
-MV = 70
-MV_TAIL = {(6, 0): 64, (6, 1): 64, (7, 0): 48, (7, 1): 48}
+MV = 80
+MV_TAIL = {(7, 1): 48}
 
 
 def tile_routed_moe_kernel(tc, xT, w1, w2, gate, offs, out):

@@ -114,8 +114,8 @@ def tile_routed_moe_kernel(tc, xT, w1, w2, gate, offs, out):
 
         def copy_w2(e, eng):
             grp2 = work3.tile([P, G * N * PACK], BF16, name="w2g", align_bytes=64)
-            dst = grp2[:].rearrange("p (g n j) -> p g n j", g=G, j=PACK)
-            src = w2r[e][:].rearrange("p g j n -> p g n j")
+            dst = grp2[:].rearrange("p (g c i j) -> p g c j i", g=G, i=4, j=PACK)
+            src = w2r[e][:].rearrange("p g j (c i) -> p g c j i", i=4)
             if eng == "S":
                 nc.scalar.copy(out=dst, in_=src)
             else:

@@ -35,7 +35,7 @@ def tile_routed_moe_kernel(tc, xT, w1, w2, gate, offs, out):
         psum_a = ctx.enter_context(tc.psum_pool(name="psum_a", bufs=4))
         psum_y = ctx.enter_context(tc.psum_pool(name="psum_y", bufs=2))
 
-        offs_t = keep.tile([P, E * C // 16], U16, name="offs_t")
+        offs_t = keep.tile([P, E * C // 16], U16, name="offs_t", align_bytes=256)
         nc.sync.dma_start(offs_t[:], offs)
 
         warm_in = keep.tile([P, 1], F32, name="warm_in")
@@ -43,7 +43,7 @@ def tile_routed_moe_kernel(tc, xT, w1, w2, gate, offs, out):
         nc.vector.memset(warm_in[:], 0.0)
         nc.scalar.activation(warm_out[:], warm_in[:], SILU)
 
-        win = keep.tile([P, T], F32, name="win")
+        win = keep.tile([P, T], F32, name="win", align_bytes=256)
         nc.vector.memset(win[:], 0.0)
 
         xv = xT.rearrange("(p j) n -> p j n", j=PACK)
@@ -51,31 +51,31 @@ def tile_routed_moe_kernel(tc, xT, w1, w2, gate, offs, out):
         gate_t = {}
 
         def load_gate(q0, q1):
-            t_ = keep.tile([P, (q1 - q0) * PAIR], F32, name="gate%d" % q0)
+            t_ = keep.tile([P, (q1 - q0) * PAIR], F32, name="gate%d" % q0, align_bytes=256)
             nc.sync.dma_start(out=t_[:], in_=gate[:, q0 * PAIR : q1 * PAIR])
             for q in range(q0, q1):
                 gate_t[q] = t_[:, (q - q0) * PAIR : (q - q0 + 1) * PAIR]
 
         def load_x(u, slot):
-            t_ = raw.tile([P, 2, T], F32, tag="slot%d" % slot, name="xr")
+            t_ = raw.tile([P, 2, T], F32, tag="slot%d" % slot, name="xr", align_bytes=256)
             nc.sync.dma_start(out=t_[:], in_=xv[:, 2 * u : 2 * u + 2, :])
             xr[u] = t_
 
         def load_w1(e, slot):
-            t_ = raw.tile([P, PACK, H], F32, tag="slot%d" % slot, name="w1r")
+            t_ = raw.tile([P, PACK, H], F32, tag="slot%d" % slot, name="w1r", align_bytes=256)
             nc.sync.dma_start(out=t_[:], in_=w1[e].rearrange("(p j) i -> p j i", j=PACK))
             for g in range(G):
                 w1r[(e, g)] = t_[:, :, g * PASS : (g + 1) * PASS]
 
         def load_w1_half(e, g, slot):
-            t_ = raw.tile([P, PACK, PASS], F32, tag="slot%d" % slot, name="w1rh")
+            t_ = raw.tile([P, PACK, PASS], F32, tag="slot%d" % slot, name="w1rh", align_bytes=256)
             nc.sync.dma_start(
                 out=t_[:], in_=w1[e][:, g * PASS : (g + 1) * PASS].rearrange("(p j) i -> p j i", j=PACK)
             )
             w1r[(e, g)] = t_[:]
 
         def load_w2(e):
-            t_ = w2raw.tile([P, G, PACK, N], F32, name="w2r")
+            t_ = w2raw.tile([P, G, PACK, N], F32, name="w2r", align_bytes=256)
             nc.sync.dma_start(out=t_[:], in_=w2[e].rearrange("(g p j) n -> p g j n", g=G, j=PACK))
             w2r[e] = t_
 
@@ -184,7 +184,7 @@ def tile_routed_moe_kernel(tc, xT, w1, w2, gate, offs, out):
                 ysb[q] = work3.tile([P, PAIR], F32, name="ysb")
                 nc.vector.tensor_copy(out=ysb[q][:], in_=py[q][:])
             else:
-                ysb[q] = raw.tile([P, PAIR], F32, tag="slot%d" % slot, name="ysb_s")
+                ysb[q] = raw.tile([P, PAIR], F32, tag="slot%d" % slot, name="ysb_s", align_bytes=256)
                 nc.scalar.copy(out=ysb[q][:], in_=py[q][:])
 
         def scatter(q):

@@ -24,6 +24,17 @@ MV = 80
 MV_TAIL = {(7, 1): 48}
 
 
+LOADS = (("x",0),("x",1),("w1",0),("w2",0),("w2",1),("gate",0,2),("w1",1),("w2",2),("w1",2),("w2",3),("w1",3),("w2",4),("w1",4),("w2",5),("w1",5),("w1h",6,0),("w1h",6,1),("w1h",7,0),("gate",2,3),("w1h",7,1),("w2",6),("w2",7),("gate",3,4))
+SHARE = [80] * 15 + [48]
+W2ENG = "SSSSSSSV"
+LATE_W2 = ()
+DEFER_HQ = ()
+TOK_HB = {6: ("w1h",7,0), 7: ("w1h",7,1)}
+TOK_HC = {}
+TOK_QC = {}
+Y_KEY = {}
+
+
 def tile_routed_moe_kernel(tc, xT, w1, w2, gate, offs, out):
     nc = tc.nc
     with ExitStack() as ctx:
@@ -49,35 +60,62 @@ def tile_routed_moe_kernel(tc, xT, w1, w2, gate, offs, out):
         xv = xT.rearrange("(p j) n -> p j n", j=PACK)
         xr, w1r, w2r = {}, {}, {}
         gate_t = {}
+        ring = [0]
+        slot_of = {}
+        freed = set()
+        busy = {}
+        pending = list(LOADS)
 
-        def load_gate(q0, q1):
-            t_ = keep.tile([P, (q1 - q0) * PAIR], F32, name="gate%d" % q0, align_bytes=256)
-            nc.sync.dma_start(out=t_[:], in_=gate[:, q0 * PAIR : q1 * PAIR])
-            for q in range(q0, q1):
-                gate_t[q] = t_[:, (q - q0) * PAIR : (q - q0 + 1) * PAIR]
+        def raw_tile(key, shape):
+            s = ring[0] % 7
+            ring[0] += 1
+            slot_of[key] = s
+            busy[s] = key
+            return raw.tile(shape, F32, tag="slot%d" % s, name="raw_" + "_".join(str(k) for k in key), align_bytes=256)
 
-        def load_x(u, slot):
-            t_ = raw.tile([P, 2, T], F32, tag="slot%d" % slot, name="xr", align_bytes=256)
-            nc.sync.dma_start(out=t_[:], in_=xv[:, 2 * u : 2 * u + 2, :])
-            xr[u] = t_
+        def ready(item):
+            if item[0] in ("w2", "gate"):
+                return True
+            s = ring[0] % 7
+            return s not in busy or busy[s] in freed
 
-        def load_w1(e, slot):
-            t_ = raw.tile([P, PACK, H], F32, tag="slot%d" % slot, name="w1r", align_bytes=256)
-            nc.sync.dma_start(out=t_[:], in_=w1[e].rearrange("(p j) i -> p j i", j=PACK))
-            for g in range(G):
-                w1r[(e, g)] = t_[:, :, g * PASS : (g + 1) * PASS]
+        def issue():
+            while pending and ready(pending[0]):
+                it = pending.pop(0)
+                if it[0] == "x":
+                    t_ = raw_tile(it, [P, 2, T])
+                    nc.sync.dma_start(out=t_[:], in_=xv[:, 2 * it[1] : 2 * it[1] + 2, :])
+                    xr[it[1]] = t_
+                elif it[0] == "w1":
+                    e = it[1]
+                    t_ = raw_tile(it, [P, PACK, H])
+                    nc.sync.dma_start(out=t_[:], in_=w1[e].rearrange("(p j) i -> p j i", j=PACK))
+                    for g in range(G):
+                        w1r[(e, g)] = t_[:, :, g * PASS : (g + 1) * PASS]
+                elif it[0] == "w1h":
+                    e, g = it[1], it[2]
+                    t_ = raw_tile(it, [P, PACK, PASS])
+                    nc.sync.dma_start(
+                        out=t_[:], in_=w1[e][:, g * PASS : (g + 1) * PASS].rearrange("(p j) i -> p j i", j=PACK)
+                    )
+                    w1r[(e, g)] = t_[:]
+                elif it[0] == "w2":
+                    t_ = w2raw.tile([P, G, PACK, N], F32, name="w2r", align_bytes=256)
+                    nc.sync.dma_start(out=t_[:], in_=w2[it[1]].rearrange("(g p j) n -> p g j n", g=G, j=PACK))
+                    w2r[it[1]] = t_
+                else:
+                    q0, q1 = it[1], it[2]
+                    t_ = keep.tile([P, (q1 - q0) * PAIR], F32, name="gate%d" % q0, align_bytes=256)
+                    nc.sync.dma_start(out=t_[:], in_=gate[:, q0 * PAIR : q1 * PAIR])
+                    for q in range(q0, q1):
+                        gate_t[q] = t_[:, (q - q0) * PAIR : (q - q0 + 1) * PAIR]
 
-        def load_w1_half(e, g, slot):
-            t_ = raw.tile([P, PACK, PASS], F32, tag="slot%d" % slot, name="w1rh", align_bytes=256)
-            nc.sync.dma_start(
-                out=t_[:], in_=w1[e][:, g * PASS : (g + 1) * PASS].rearrange("(p j) i -> p j i", j=PACK)
-            )
-            w1r[(e, g)] = t_[:]
+        def free(key):
+            freed.add(key)
+            issue()
 
-        def load_w2(e):
-            t_ = w2raw.tile([P, G, PACK, N], F32, name="w2r", align_bytes=256)
-            nc.sync.dma_start(out=t_[:], in_=w2[e].rearrange("(g p j) n -> p g j n", g=G, j=PACK))
-            w2r[e] = t_
+        def token(slotkey, width, dtype, name):
+            return raw.tile([P, width], dtype, tag="slot%d" % slot_of[slotkey], name=name, align_bytes=256)
 
         xb = [keep.tile([P, 2 * T], BF16, name="xb%d" % u) for u in range(2)]
         xg = keep.tile([P, E * C * PACK], BF16, name="xg", align_bytes=64)
@@ -107,9 +145,12 @@ def tile_routed_moe_kernel(tc, xT, w1, w2, gate, offs, out):
             w1g[(e, g)] = grp
 
         def quant_w1(e, g):
-            c_ = work4.tile([P, PASS], U32, name="w1c", align_bytes=64)
+            if (e, g) in TOK_QC:
+                c_ = token(TOK_QC[(e, g)], PASS, U32, "w1c_s")[:]
+            else:
+                c_ = work4.tile([P, PASS], U32, name="w1c", align_bytes=64)
             s_ = work4.tile([P, PASS], U8, name="w1s", align_bytes=64)
-            nc.vector.quantize_mx(out=c_[:].bitcast(FP8X4), scales=s_[:], in_=w1g[(e, g)][:])
+            nc.vector.quantize_mx(out=(c_ if (e, g) in TOK_QC else c_[:]).bitcast(FP8X4), scales=s_[:], in_=w1g[(e, g)][:])
             w1c[(e, g)], w1s[(e, g)] = c_, s_
 
         def copy_w2(e, eng):
@@ -146,8 +187,12 @@ def tile_routed_moe_kernel(tc, xT, w1, w2, gate, offs, out):
 
         def silu(e, g):
             if g == 0:
-                hb[e] = work3.tile([P, G * C * PACK], BF16, name="hb", align_bytes=64)
-                hc[e] = work3.tile([P, G * C], U32, name="hc", align_bytes=64)
+                if e in TOK_HB:
+                    hb[e] = token(TOK_HB[e], G * C * PACK, BF16, "hb_s")
+                else:
+                    hb[e] = work3.tile([P, G * C * PACK], BF16, name="hb", align_bytes=64)
+                if e not in TOK_HC:
+                    hc[e] = work3.tile([P, G * C], U32, name="hc", align_bytes=64)
                 hs[e] = work3.tile([P, G * C], U8, name="hs", align_bytes=64)
             nc.scalar.activation(
                 hb[e][:, g * C * PACK : (g + 1) * C * PACK].rearrange("p (s t) -> p s t", t=PACK),
@@ -156,6 +201,8 @@ def tile_routed_moe_kernel(tc, xT, w1, w2, gate, offs, out):
             )
 
         def quant_h(e, gs):
+            if e not in hc:
+                hc[e] = token(TOK_HC[e], G * C, U32, "hc_s")
             a, b = gs[0], gs[-1] + 1
             nc.vector.quantize_mx(
                 out=hc[e][:, a * C : b * C].bitcast(FP8X4),
@@ -181,72 +228,75 @@ def tile_routed_moe_kernel(tc, xT, w1, w2, gate, offs, out):
 
         def ycopy(q, slot):
             if slot is None:
-                ysb[q] = work3.tile([P, PAIR], F32, name="ysb")
-                nc.vector.tensor_copy(out=ysb[q][:], in_=py[q][:])
+                ysb[q] = work3.tile([P, PAIR], F32, name="ysb")[:]
+                nc.vector.tensor_copy(out=ysb[q], in_=py[q][:])
             else:
-                ysb[q] = raw.tile([P, PAIR], F32, tag="slot%d" % slot, name="ysb_s", align_bytes=256)
-                nc.scalar.copy(out=ysb[q][:], in_=py[q][:])
+                ysb[q] = token(slot, PAIR, F32, "ysb_s")[:]
+                nc.scalar.copy(out=ysb[q], in_=py[q][:])
 
         def scatter(q):
             nc.vector.tensor_tensor(
                 win[:].indirect(offs_t[:, q * (PAIR // 16) : (q + 1) * (PAIR // 16)]),
-                ysb[q][:],
+                ysb[q],
                 gate_t[q],
                 MULT,
             )
 
-        load_x(0, 0)
-        load_x(1, 1)
-        load_w1(0, 4)
-        load_w2(0)
-        load_w2(1)
-        load_gate(0, 2)
-        load_w1(1, 5)
-        load_w2(2)
-        load_w1(2, 6)
+        issue()
 
         for u in range(2):
             cast_x(u, 0, XV, "V")
             cast_x(u, XV, T, "S")
             gather_x(u)
+            free(("x", u))
         nc.vector.quantize_mx(out=xc[:].bitcast(FP8X4), scales=xs[:], in_=xg[:])
 
-        load_w2(3)
-        load_w1(3, 0)
-        load_w2(4)
-        load_w1(4, 1)
-        load_w2(5)
-        load_w1(5, 2)
-        load_w1(6, 3)
 
-        y_slot = {0: 6, 1: 1, 2: 3}
+        def rawkey(e, g):
+            return ("w1", e) if ("w1", e) in LOADS else ("w1h", e, g)
+
+        def free_piece(e, g):
+            k = rawkey(e, g)
+            if k[0] == "w1" and g == 0:
+                return
+            free(k)
+
+        def layer2(e):
+            quant_w2(e)
+            mm2(e)
+
         for e in range(E):
-            copy_w1(e, 0, MV_TAIL.get((e, 0), MV))
-            copy_w1(e, 1, MV_TAIL.get((e, 1), MV))
-            if e == 0:
-                load_gate(2, 3)
-            if e == 1:
-                load_w1_half(7, 0, 5)
+            copy_w1(e, 0, SHARE[2 * e])
+            if e < 7:
+                free_piece(e, 0)
+            copy_w1(e, 1, SHARE[2 * e + 1])
+            if e in DEFER_HQ:
+                pass
+            if e - 1 in DEFER_HQ:
+                quant_h(e - 1, (0, 1))
+                mm2(e - 1)
             if e % 2 == 0 and e > 0:
-                q = e // 2 - 1
-                ycopy(q, y_slot[q])
-                scatter(q)
-                if q == 0:
-                    load_w1_half(7, 1, 6)
-                    load_w2(6)
-                    load_w2(7)
-                    load_gate(3, 4)
-            copy_w2(e, "V" if e == 7 else "S")
+                ycopy(e // 2 - 1, Y_KEY.get(e // 2 - 1, rawkey(e, 1)))
+                scatter(e // 2 - 1)
+            free_piece(e, 1)
+            if e not in LATE_W2:
+                copy_w2(e, W2ENG[e])
             for g in range(G):
                 quant_w1(e, g)
                 mm1(e, g)
-            quant_w2(e)
+            if e not in LATE_W2:
+                quant_w2(e)
             for g in range(G):
                 silu(e, g)
                 if e == E - 1:
                     quant_h(e, (g,))
-            if e < E - 1:
+            if e < E - 1 and e not in DEFER_HQ:
                 quant_h(e, (0, 1))
+            if e not in LATE_W2 and e not in DEFER_HQ:
+                mm2(e)
+        for e in LATE_W2:
+            copy_w2(e, W2ENG[e])
+            quant_w2(e)
             mm2(e)
         ycopy(3, None)
         scatter(3)

@@ -12,6 +12,7 @@ U16 = mybir.dt.uint16
 U8 = mybir.dt.uint8
 FP8X4 = mybir.dt.float8_e4m3fn_x4
 SILU = mybir.ActivationFunctionType.Silu
+COPY = mybir.ActivationFunctionType.Copy
 MULT = mybir.AluOpType.mult
 
 P = 128
@@ -24,15 +25,37 @@ MV = 80
 MV_TAIL = {(7, 1): 48}
 
 
-LOADS = (("x",0),("x",1),("w1",0),("w2",0),("w2",1),("gate",0,2),("w1",1),("w2",2),("w1",2),("w2",3),("w1",3),("w2",4),("w1",4),("w2",5),("w1",5),("w1h",6,0),("w1h",6,1),("w1h",7,0),("gate",2,3),("w1h",7,1),("w2",6),("w2",7),("gate",3,4))
+LOADS = (("x",0),("x",1),("w1",0),("w2",0),("w2",1),("gate",0,2),("w1",1),("w2",2),("w1",2),("w2",3),("w1",3),("w2",4),("w1",4),("w2",5),("w1",5),("w1h",6,0),("w1h",6,1),("gate",2,3),("w1h",7,0),("w1h",7,1),("w2",6),("w2",7),("gate",3,4))
 SHARE = [80] * 15 + [48]
 W2ENG = "SSSSSSSV"
 LATE_W2 = ()
 DEFER_HQ = ()
-TOK_HB = {6: ("w1h",7,0), 7: ("w1h",7,1)}
+TOK_HB = {}
 TOK_HC = {}
 TOK_QC = {}
 Y_KEY = {}
+
+
+WBUF = 4
+
+
+def WTAG(e, g):
+    return "w1g"
+
+
+ORDER = ("c00","c10","y_0","sc0","wc0","q00","q10","wq0","s00","s10","hq0","m20","fr0")
+LAST_ORDER = ("c00", "c10", "y_0", "sc0", "fr0", "wc0", "q00", "q10", "wq0", "s00", "s10", "hq0", "m20")
+LAST_FROM = 99
+HALF_HQ = (7,)
+
+
+Y_STAGE = (2,4,6)
+Y_PIECE = 1
+PSY = 2
+
+
+S_TOK = ((6, 0), (7, 0), (7, 1))
+HB_S = {5: (6, 0), 6: (7, 0), 7: (7, 1)}
 
 
 def tile_routed_moe_kernel(tc, xT, w1, w2, gate, offs, out):
@@ -40,11 +63,11 @@ def tile_routed_moe_kernel(tc, xT, w1, w2, gate, offs, out):
     with ExitStack() as ctx:
         keep = ctx.enter_context(tc.tile_pool(name="keep", bufs=1))
         raw = ctx.enter_context(tc.tile_pool(name="raw", bufs=1))
-        w2raw = ctx.enter_context(tc.tile_pool(name="w2raw", bufs=E))
+        w2raw = ctx.enter_context(tc.tile_pool(name="w2raw", bufs=6))
         work4 = ctx.enter_context(tc.tile_pool(name="work4", bufs=4))
         work3 = ctx.enter_context(tc.tile_pool(name="work3", bufs=3))
         psum_a = ctx.enter_context(tc.psum_pool(name="psum_a", bufs=4))
-        psum_y = ctx.enter_context(tc.psum_pool(name="psum_y", bufs=2))
+        psum_y = ctx.enter_context(tc.psum_pool(name="psum_y", bufs=PSY))
 
         offs_t = keep.tile([P, E * C // 16], U16, name="offs_t", align_bytes=256)
         nc.sync.dma_start(offs_t[:], offs)
@@ -53,6 +76,11 @@ def tile_routed_moe_kernel(tc, xT, w1, w2, gate, offs, out):
         warm_out = keep.tile([P, 1], F32, name="warm_out")
         nc.vector.memset(warm_in[:], 0.0)
         nc.scalar.activation(warm_out[:], warm_in[:], SILU)
+
+        tk = {}
+        for key in S_TOK:
+            tk[key] = keep.tile([P, 1], F32, tag="tk%d%d" % key, name="tk", align_bytes=256)
+            nc.gpsimd.memset(tk[key][:], 1.0)
 
         win = keep.tile([P, T], F32, name="win", align_bytes=256)
         nc.vector.memset(win[:], 0.0)
@@ -137,11 +165,15 @@ def tile_routed_moe_kernel(tc, xT, w1, w2, gate, offs, out):
         w1g, w1c, w1s, w2g, w2c, w2s, pa, hb, hc, hs, py, ysb = {}, {}, {}, {}, {}, {}, {}, {}, {}, {}, {}, {}
 
         def copy_w1(e, g, mv):
-            grp = work4.tile([P, PACK * PASS], BF16, name="w1g", align_bytes=64)
+            grp = work4.tile([P, PACK * PASS], BF16, name="w1g", tag=WTAG(e, g), bufs=WBUF, align_bytes=64)
             dst = grp[:].rearrange("p (t m j) -> p m j t", t=PACK, j=PACK)
             src = w1r[(e, g)].rearrange("p j (m t) -> p m j t", t=PACK)
-            nc.vector.tensor_copy(out=dst[:, 0:mv], in_=src[:, 0:mv])
-            nc.scalar.copy(out=dst[:, mv:P], in_=src[:, mv:P])
+            if mv > 0:
+                nc.vector.tensor_copy(out=dst[:, 0:mv], in_=src[:, 0:mv])
+            if mv < P and (e, g) in S_TOK:
+                nc.scalar.activation(dst[:, mv:P], src[:, mv:P], COPY, scale=tk[(e, g)][:])
+            elif mv < P:
+                nc.scalar.copy(out=dst[:, mv:P], in_=src[:, mv:P])
             w1g[(e, g)] = grp
 
         def quant_w1(e, g):
@@ -187,7 +219,9 @@ def tile_routed_moe_kernel(tc, xT, w1, w2, gate, offs, out):
 
         def silu(e, g):
             if g == 0:
-                if e in TOK_HB:
+                if e in HB_S:
+                    hb[e] = keep.tile([P, G * C * PACK], BF16, tag="tk%d%d" % HB_S[e], name="hb_k", align_bytes=256)
+                elif e in TOK_HB:
                     hb[e] = token(TOK_HB[e], G * C * PACK, BF16, "hb_s")
                 else:
                     hb[e] = work3.tile([P, G * C * PACK], BF16, name="hb", align_bytes=64)
@@ -228,7 +262,7 @@ def tile_routed_moe_kernel(tc, xT, w1, w2, gate, offs, out):
 
         def ycopy(q, slot):
             if slot is None:
-                ysb[q] = work3.tile([P, PAIR], F32, name="ysb")[:]
+                ysb[q] = keep.tile([P, PAIR], F32, name="ysb")[:]
                 nc.vector.tensor_copy(out=ysb[q], in_=py[q][:])
             else:
                 ysb[q] = token(slot, PAIR, F32, "ysb_s")[:]
@@ -265,39 +299,50 @@ def tile_routed_moe_kernel(tc, xT, w1, w2, gate, offs, out):
             quant_w2(e)
             mm2(e)
 
-        for e in range(E):
-            copy_w1(e, 0, SHARE[2 * e])
-            if e < 7:
-                free_piece(e, 0)
-            copy_w1(e, 1, SHARE[2 * e + 1])
-            if e in DEFER_HQ:
-                pass
-            if e - 1 in DEFER_HQ:
-                quant_h(e - 1, (0, 1))
-                mm2(e - 1)
-            if e % 2 == 0 and e > 0:
-                ycopy(e // 2 - 1, Y_KEY.get(e // 2 - 1, rawkey(e, 1)))
-                scatter(e // 2 - 1)
-            free_piece(e, 1)
-            if e not in LATE_W2:
+        def stage(s, e):
+            if s == "c0":
+                copy_w1(e, 0, SHARE[2 * e])
+                if e < 7:
+                    free_piece(e, 0)
+            elif s == "c1":
+                copy_w1(e, 1, SHARE[2 * e + 1])
+            elif s == "y_":
+                if e in Y_STAGE:
+                    ycopy(Y_STAGE.index(e), rawkey(e, Y_PIECE))
+            elif s == "sc":
+                if e in Y_STAGE:
+                    scatter(Y_STAGE.index(e))
+            elif s == "fr":
+                free_piece(e, 1)
+            elif s == "wc":
                 copy_w2(e, W2ENG[e])
-            for g in range(G):
-                quant_w1(e, g)
-                mm1(e, g)
-            if e not in LATE_W2:
+            elif s == "q0":
+                quant_w1(e, 0)
+                mm1(e, 0)
+            elif s == "q1":
+                quant_w1(e, 1)
+                mm1(e, 1)
+            elif s == "wq":
                 quant_w2(e)
-            for g in range(G):
-                silu(e, g)
-                if e == E - 1:
-                    quant_h(e, (g,))
-            if e < E - 1 and e not in DEFER_HQ:
-                quant_h(e, (0, 1))
-            if e not in LATE_W2 and e not in DEFER_HQ:
+            elif s == "s0":
+                silu(e, 0)
+                if e in HALF_HQ:
+                    quant_h(e, (0,))
+            elif s == "s1":
+                silu(e, 1)
+                if e in HALF_HQ:
+                    quant_h(e, (1,))
+            elif s == "hq":
+                if e not in HALF_HQ:
+                    quant_h(e, (0, 1))
+            elif s == "m2":
                 mm2(e)
-        for e in LATE_W2:
-            copy_w2(e, W2ENG[e])
-            quant_w2(e)
-            mm2(e)
+
+        for step in range(E + 2):
+            for s in (LAST_ORDER if step >= LAST_FROM else ORDER):
+                e = step - int(s[2:])
+                if 0 <= e < E:
+                    stage(s[:2], e)
         ycopy(3, None)
         scatter(3)
 

@@ -58,12 +58,22 @@ S_TOK = ((6, 0), (7, 0), (7, 1))
 HB_S = {5: (6, 0), 6: (7, 0), 7: (7, 1)}
 
 
+SILU_TOK = ()
+W2_S = {}
+
+
+W2_MERGE = False
+
+
+W2BUF = 4
+
+
 def tile_routed_moe_kernel(tc, xT, w1, w2, gate, offs, out):
     nc = tc.nc
     with ExitStack() as ctx:
         keep = ctx.enter_context(tc.tile_pool(name="keep", bufs=1))
         raw = ctx.enter_context(tc.tile_pool(name="raw", bufs=1))
-        w2raw = ctx.enter_context(tc.tile_pool(name="w2raw", bufs=6))
+        w2raw = ctx.enter_context(tc.tile_pool(name="w2raw", bufs=W2BUF))
         work4 = ctx.enter_context(tc.tile_pool(name="work4", bufs=4))
         work3 = ctx.enter_context(tc.tile_pool(name="work3", bufs=3))
         psum_a = ctx.enter_context(tc.psum_pool(name="psum_a", bufs=4))
@@ -77,16 +87,23 @@ def tile_routed_moe_kernel(tc, xT, w1, w2, gate, offs, out):
         nc.vector.memset(warm_in[:], 0.0)
         nc.scalar.activation(warm_out[:], warm_in[:], SILU)
 
+        w2pairs = []
+        ones = keep.tile([P, 1], F32, name="ones")
+        nc.vector.memset(ones[:], 1.0)
+        stk = {}
+        for key in SILU_TOK:
+            stk[key] = keep.tile([P, 1], F32, tag="stk%d%d" % key, name="stk", align_bytes=256)
+            nc.scalar.copy(out=stk[key][:], in_=ones[:])
         tk = {}
         for key in S_TOK:
             tk[key] = keep.tile([P, 1], F32, tag="tk%d%d" % key, name="tk", align_bytes=256)
-            nc.gpsimd.memset(tk[key][:], 1.0)
+            nc.scalar.copy(out=tk[key][:], in_=ones[:])
 
         win = keep.tile([P, T], F32, name="win", align_bytes=256)
         nc.vector.memset(win[:], 0.0)
 
         xv = xT.rearrange("(p j) n -> p j n", j=PACK)
-        xr, w1r, w2r = {}, {}, {}
+        xr, w1r, w2r, w2g = {}, {}, {}, {}
         gate_t = {}
         ring = [0]
         slot_of = {}
@@ -102,8 +119,10 @@ def tile_routed_moe_kernel(tc, xT, w1, w2, gate, offs, out):
             return raw.tile(shape, F32, tag="slot%d" % s, name="raw_" + "_".join(str(k) for k in key), align_bytes=256)
 
         def ready(item):
-            if item[0] in ("w2", "gate"):
+            if item[0] == "gate":
                 return True
+            if item[0] == "w2":
+                return item[1] < W2BUF or item[1] - W2BUF in w2g
             s = ring[0] % 7
             return s not in busy or busy[s] in freed
 
@@ -162,7 +181,7 @@ def tile_routed_moe_kernel(tc, xT, w1, w2, gate, offs, out):
         def gather_x(u):
             nc.vector.tensor_copy(out=xg_words[:, :, u], in_=xb[u][:].bitcast(U32).indirect(offs_t[:]))
 
-        w1g, w1c, w1s, w2g, w2c, w2s, pa, hb, hc, hs, py, ysb = {}, {}, {}, {}, {}, {}, {}, {}, {}, {}, {}, {}
+        w1g, w1c, w1s, w2c, w2s, pa, hb, hc, hs, py, ysb = {}, {}, {}, {}, {}, {}, {}, {}, {}, {}, {}
 
         def copy_w1(e, g, mv):
             grp = work4.tile([P, PACK * PASS], BF16, name="w1g", tag=WTAG(e, g), bufs=WBUF, align_bytes=64)
@@ -186,14 +205,34 @@ def tile_routed_moe_kernel(tc, xT, w1, w2, gate, offs, out):
             w1c[(e, g)], w1s[(e, g)] = c_, s_
 
         def copy_w2(e, eng):
-            grp2 = work3.tile([P, G * N * PACK], BF16, name="w2g", align_bytes=64)
-            dst = grp2[:].rearrange("p (g c i j) -> p g c j i", g=G, i=4, j=PACK)
+            if W2_MERGE and e == 7:
+                grp2 = w2pairs[0]
+            elif e in W2_S:
+                grp2 = keep.tile([P, (2 if W2_MERGE else 1) * G * N * PACK], BF16, tag="stk%d%d" % W2_S[e], name="w2g_k", align_bytes=256)
+            else:
+                grp2 = work3.tile([P, G * N * PACK], BF16, name="w2g", align_bytes=64)
+            half = grp2[:]
+            if W2_MERGE and e == 6:
+                w2pairs.append(grp2)
+                half = grp2[:, 0 : G * N * PACK]
+            elif W2_MERGE and e == 7:
+                half = grp2[:, G * N * PACK : 2 * G * N * PACK]
+            dst = half.rearrange("p (g c i j) -> p g c j i", g=G, i=4, j=PACK)
             src = w2r[e][:].rearrange("p g j (c i) -> p g c j i", i=4)
             if eng == "S":
                 nc.scalar.copy(out=dst, in_=src)
             else:
                 nc.vector.tensor_copy(out=dst, in_=src)
             w2g[e] = grp2
+            issue()
+
+        def quant_w2_pair():
+            c_ = work3.tile([P, 2 * G * N], U32, name="w2cp", bufs=1, align_bytes=64)
+            s_ = work3.tile([P, 2 * G * N], U8, name="w2sp", bufs=1, align_bytes=64)
+            nc.vector.quantize_mx(out=c_[:].bitcast(FP8X4), scales=s_[:], in_=w2pairs[0][:])
+            for k in range(2):
+                w2c[6 + k] = c_[:, k * G * N : (k + 1) * G * N]
+                w2s[6 + k] = s_[:, k * G * N : (k + 1) * G * N]
 
         def quant_w2(e):
             c_ = work3.tile([P, G * N], U32, name="w2c", align_bytes=64)
@@ -228,11 +267,12 @@ def tile_routed_moe_kernel(tc, xT, w1, w2, gate, offs, out):
                 if e not in TOK_HC:
                     hc[e] = work3.tile([P, G * C], U32, name="hc", align_bytes=64)
                 hs[e] = work3.tile([P, G * C], U8, name="hs", align_bytes=64)
-            nc.scalar.activation(
-                hb[e][:, g * C * PACK : (g + 1) * C * PACK].rearrange("p (s t) -> p s t", t=PACK),
-                pa[(e, g)][:].rearrange("p t s -> p s t"),
-                SILU,
-            )
+            dst = hb[e][:, g * C * PACK : (g + 1) * C * PACK].rearrange("p (s t) -> p s t", t=PACK)
+            src = pa[(e, g)][:].rearrange("p t s -> p s t")
+            if (e, g) in SILU_TOK:
+                nc.scalar.activation(dst, src, SILU, scale=stk[(e, g)][:])
+            else:
+                nc.scalar.activation(dst, src, SILU)
 
         def quant_h(e, gs):
             if e not in hc:
@@ -323,7 +363,10 @@ def tile_routed_moe_kernel(tc, xT, w1, w2, gate, offs, out):
                 quant_w1(e, 1)
                 mm1(e, 1)
             elif s == "wq":
-                quant_w2(e)
+                if not (W2_MERGE and e >= 6):
+                    quant_w2(e)
+                elif e == 7:
+                    quant_w2_pair()
             elif s == "s0":
                 silu(e, 0)
                 if e in HALF_HQ:
@@ -336,7 +379,9 @@ def tile_routed_moe_kernel(tc, xT, w1, w2, gate, offs, out):
                 if e not in HALF_HQ:
                     quant_h(e, (0, 1))
             elif s == "m2":
-                mm2(e)
+                if not (W2_MERGE and e == 6):
+                    mm2(e - 1) if W2_MERGE and e == 7 else None
+                    mm2(e)
 
         for step in range(E + 2):
             for s in (LAST_ORDER if step >= LAST_FROM else ORDER):

@@ -25,7 +25,7 @@ MV = 80
 MV_TAIL = {(7, 1): 48}
 
 
-LOADS = (("x",0),("x",1),("w1",0),("w2",0),("w2",1),("gate",0,2),("w1",1),("w2",2),("w1",2),("w2",3),("w1",3),("w2",4),("w1",4),("w2",5),("w1",5),("w1h",6,0),("w1h",6,1),("gate",2,3),("w1h",7,0),("w1h",7,1),("w2",6),("w2",7),("gate",3,4))
+LOADS = (("x",0),("x",1),("w1",0),("w2",0),("w2",1),("gate",0,2),("w1",1),("w2",2),("w1",2),("w2",3),("w1",3),("w2",4),("w1",4),("w2",5),("w1",5),("w1h",6,0),("w1h",6,1),("w1h",7,0),("gate",2,3),("w1h",7,1),("w2",6),("w2",7),("gate",3,4))
 SHARE = [80] * 15 + [48]
 W2ENG = "SSSSSSSV"
 LATE_W2 = ()
@@ -65,7 +65,13 @@ W2_S = {}
 W2_MERGE = False
 
 
-W2BUF = 4
+W2BUF = 6
+
+
+LASTSPLIT = False
+
+
+LASTENG = "V"
 
 
 def tile_routed_moe_kernel(tc, xT, w1, w2, gate, offs, out):
@@ -285,13 +291,17 @@ def tile_routed_moe_kernel(tc, xT, w1, w2, gate, offs, out):
             )
 
         def mm2(e):
-            if e % 2 == 0:
-                py[e // 2] = psum_y.tile([P, PAIR], F32, name="py")
-            half = slice((e % 2) * C, (e % 2 + 1) * C)
+            if e >= 6 and LASTSPLIT:
+                py[("last", e)] = psum_y.tile([P, C], F32, name="pyl", bufs=1, tag="pyl%d" % e)
+                bank = py[("last", e)][:]
+            else:
+                if e % 2 == 0:
+                    py[e // 2] = psum_y.tile([P, PAIR], F32, name="py")
+                bank = py[e // 2][:, (e % 2) * C : (e % 2 + 1) * C]
             for g in range(G):
                 cols = slice(g * P, (g + 1) * P)
                 nc.tensor.matmul_mx(
-                    out=py[e // 2][:, half],
+                    out=bank,
                     lhsT=w2c[e][:, cols].bitcast(FP8X4),
                     lhsT_scale=w2s[e][:, cols],
                     rhs=hc[e][:, cols].bitcast(FP8X4),
@@ -303,7 +313,10 @@ def tile_routed_moe_kernel(tc, xT, w1, w2, gate, offs, out):
         def ycopy(q, slot):
             if slot is None:
                 ysb[q] = keep.tile([P, PAIR], F32, name="ysb")[:]
-                nc.vector.tensor_copy(out=ysb[q], in_=py[q][:])
+                if LASTENG == "S":
+                    nc.scalar.copy(out=ysb[q], in_=py[q][:])
+                else:
+                    nc.vector.tensor_copy(out=ysb[q], in_=py[q][:])
             else:
                 ysb[q] = token(slot, PAIR, F32, "ysb_s")[:]
                 nc.scalar.copy(out=ysb[q], in_=py[q][:])
@@ -388,7 +401,15 @@ def tile_routed_moe_kernel(tc, xT, w1, w2, gate, offs, out):
                 e = step - int(s[2:])
                 if 0 <= e < E:
                     stage(s[:2], e)
-        ycopy(3, None)
+        if LASTSPLIT:
+            ysb[3] = keep.tile([P, PAIR], F32, name="ysb")[:]
+            nc.scalar.copy(out=ysb[3][:, 0:C], in_=py[("last", 6)][:])
+            if LASTENG == "S":
+                nc.scalar.copy(out=ysb[3][:, C:PAIR], in_=py[("last", 7)][:])
+            else:
+                nc.vector.tensor_copy(out=ysb[3][:, C:PAIR], in_=py[("last", 7)][:])
+        else:
+            ycopy(3, None)
         scatter(3)
 
         nc.sync.dma_start(out=out, in_=win[:])

from contextlib import ExitStack

import concourse.mybir as mybir

K, T, E, C, H, N = 512, 2048, 8, 128, 1024, 128
FLOPS = 2 * E * C * (K * H + H * N)

F32 = mybir.dt.float32
BF16 = mybir.dt.bfloat16
U32 = mybir.dt.uint32
U16 = mybir.dt.uint16
U8 = mybir.dt.uint8
FP8X4 = mybir.dt.float8_e4m3fn_x4
SILU = mybir.ActivationFunctionType.Silu
COPY = mybir.ActivationFunctionType.Copy
MULT = mybir.AluOpType.mult

P = 128
PACK = 4
PASS = P * PACK
G = H // PASS
PAIR = 2 * C
XV = 1344
MV = 80
MV_TAIL = {(7, 1): 48}


LOADS = (("x",0),("x",1),("w1",0),("w2",0),("w2",1),("gate",0,2),("w1",1),("w2",2),("w1",2),("w2",3),("w1",3),("w2",4),("w1",4),("w2",5),("w1",5),("w1h",6,0),("w1h",6,1),("w1h",7,0),("gate",2,3),("w1h",7,1),("w2",6),("w2",7),("gate",3,4))
SHARE = [80] * 15 + [48]
W2ENG = "SSSSSSSV"
LATE_W2 = ()
DEFER_HQ = ()
TOK_HB = {}
TOK_HC = {}
TOK_QC = {}
Y_KEY = {}


WBUF = 4


def WTAG(e, g):
    return "w1g"


ORDER = ("c00","c10","y_0","sc0","wc0","q00","q10","wq0","s00","s10","hq0","m20","fr0")
LAST_ORDER = ("c00", "c10", "y_0", "sc0", "fr0", "wc0", "q00", "q10", "wq0", "s00", "s10", "hq0", "m20")
LAST_FROM = 99
HALF_HQ = (7,)


Y_STAGE = (2,4,6)
Y_PIECE = 1
PSY = 2


S_TOK = ((6, 0), (7, 0), (7, 1))
HB_S = {5: (6, 0), 6: (7, 0), 7: (7, 1)}


SILU_TOK = ()
W2_S = {}


W2_MERGE = False


W2BUF = 6


LASTSPLIT = False


LASTENG = "V"


def tile_routed_moe_kernel(tc, xT, w1, w2, gate, offs, out):
    nc = tc.nc
    with ExitStack() as ctx:
        keep = ctx.enter_context(tc.tile_pool(name="keep", bufs=1))
        raw = ctx.enter_context(tc.tile_pool(name="raw", bufs=1))
        w2raw = ctx.enter_context(tc.tile_pool(name="w2raw", bufs=W2BUF))
        work4 = ctx.enter_context(tc.tile_pool(name="work4", bufs=4))
        work3 = ctx.enter_context(tc.tile_pool(name="work3", bufs=3))
        psum_a = ctx.enter_context(tc.psum_pool(name="psum_a", bufs=4))
        psum_y = ctx.enter_context(tc.psum_pool(name="psum_y", bufs=PSY))

        offs_t = keep.tile([P, E * C // 16], U16, name="offs_t", align_bytes=256)
        nc.sync.dma_start(offs_t[:], offs)

        warm_in = keep.tile([P, 1], F32, name="warm_in")
        warm_out = keep.tile([P, 1], F32, name="warm_out")
        nc.vector.memset(warm_in[:], 0.0)
        nc.scalar.activation(warm_out[:], warm_in[:], SILU)

        w2pairs = []
        ones = keep.tile([P, 1], F32, name="ones")
        nc.vector.memset(ones[:], 1.0)
        stk = {}
        for key in SILU_TOK:
            stk[key] = keep.tile([P, 1], F32, tag="stk%d%d" % key, name="stk", align_bytes=256)
            nc.scalar.copy(out=stk[key][:], in_=ones[:])
        tk = {}
        for key in S_TOK:
            tk[key] = keep.tile([P, 1], F32, tag="tk%d%d" % key, name="tk", align_bytes=256)
            nc.scalar.copy(out=tk[key][:], in_=ones[:])

        win = keep.tile([P, T], F32, name="win", align_bytes=256)
        nc.vector.memset(win[:], 0.0)

        xv = xT.rearrange("(p j) n -> p j n", j=PACK)
        xr, w1r, w2r, w2g = {}, {}, {}, {}
        gate_t = {}
        ring = [0]
        slot_of = {}
        freed = set()
        busy = {}
        pending = list(LOADS)

        def raw_tile(key, shape):
            s = ring[0] % 7
            ring[0] += 1
            slot_of[key] = s
            busy[s] = key
            return raw.tile(shape, F32, tag="slot%d" % s, name="raw_" + "_".join(str(k) for k in key), align_bytes=256)

        def ready(item):
            if item[0] == "gate":
                return True
            if item[0] == "w2":
                return item[1] < W2BUF or item[1] - W2BUF in w2g
            s = ring[0] % 7
            return s not in busy or busy[s] in freed

        def issue():
            while pending and ready(pending[0]):
                it = pending.pop(0)
                if it[0] == "x":
                    t_ = raw_tile(it, [P, 2, T])
                    nc.sync.dma_start(out=t_[:], in_=xv[:, 2 * it[1] : 2 * it[1] + 2, :])
                    xr[it[1]] = t_
                elif it[0] == "w1":
                    e = it[1]
                    t_ = raw_tile(it, [P, PACK, H])
                    nc.sync.dma_start(out=t_[:], in_=w1[e].rearrange("(p j) i -> p j i", j=PACK))
                    for g in range(G):
                        w1r[(e, g)] = t_[:, :, g * PASS : (g + 1) * PASS]
                elif it[0] == "w1h":
                    e, g = it[1], it[2]
                    t_ = raw_tile(it, [P, PACK, PASS])
                    nc.sync.dma_start(
                        out=t_[:], in_=w1[e][:, g * PASS : (g + 1) * PASS].rearrange("(p j) i -> p j i", j=PACK)
                    )
                    w1r[(e, g)] = t_[:]
                elif it[0] == "w2":
                    t_ = w2raw.tile([P, G, PACK, N], F32, name="w2r", align_bytes=256)
                    nc.sync.dma_start(out=t_[:], in_=w2[it[1]].rearrange("(g p j) n -> p g j n", g=G, j=PACK))
                    w2r[it[1]] = t_
                else:
                    q0, q1 = it[1], it[2]
                    t_ = keep.tile([P, (q1 - q0) * PAIR], F32, name="gate%d" % q0, align_bytes=256)
                    nc.sync.dma_start(out=t_[:], in_=gate[:, q0 * PAIR : q1 * PAIR])
                    for q in range(q0, q1):
                        gate_t[q] = t_[:, (q - q0) * PAIR : (q - q0 + 1) * PAIR]

        def free(key):
            freed.add(key)
            issue()

        def token(slotkey, width, dtype, name):
            return raw.tile([P, width], dtype, tag="slot%d" % slot_of[slotkey], name=name, align_bytes=256)

        xb = [keep.tile([P, 2 * T], BF16, name="xb%d" % u) for u in range(2)]
        xg = keep.tile([P, E * C * PACK], BF16, name="xg", align_bytes=64)
        xg_words = xg[:].bitcast(U32).rearrange("p (s u) -> p s u", u=2)
        xc = keep.tile([P, E * C], U32, name="xc", align_bytes=64)
        xs = keep.tile([P, E * C], U8, name="xs", align_bytes=64)

        def cast_x(u, a, b, eng):
            dst = xb[u][:, 2 * a : 2 * b].rearrange("p (n e) -> p n e", e=2)
            src = xr[u][:, :, a:b].rearrange("p e n -> p n e")
            if eng == "S":
                nc.scalar.copy(out=dst, in_=src)
            else:
                nc.vector.tensor_copy(out=dst, in_=src)

        def gather_x(u):
            nc.vector.tensor_copy(out=xg_words[:, :, u], in_=xb[u][:].bitcast(U32).indirect(offs_t[:]))

        w1g, w1c, w1s, w2c, w2s, pa, hb, hc, hs, py, ysb = {}, {}, {}, {}, {}, {}, {}, {}, {}, {}, {}

        def copy_w1(e, g, mv):
            grp = work4.tile([P, PACK * PASS], BF16, name="w1g", tag=WTAG(e, g), bufs=WBUF, align_bytes=64)
            dst = grp[:].rearrange("p (t m j) -> p m j t", t=PACK, j=PACK)
            src = w1r[(e, g)].rearrange("p j (m t) -> p m j t", t=PACK)
            if mv > 0:
                nc.vector.tensor_copy(out=dst[:, 0:mv], in_=src[:, 0:mv])
            if mv < P and (e, g) in S_TOK:
                nc.scalar.activation(dst[:, mv:P], src[:, mv:P], COPY, scale=tk[(e, g)][:])
            elif mv < P:
                nc.scalar.copy(out=dst[:, mv:P], in_=src[:, mv:P])
            w1g[(e, g)] = grp

        def quant_w1(e, g):
            if (e, g) in TOK_QC:
                c_ = token(TOK_QC[(e, g)], PASS, U32, "w1c_s")[:]
            else:
                c_ = work4.tile([P, PASS], U32, name="w1c", align_bytes=64)
            s_ = work4.tile([P, PASS], U8, name="w1s", align_bytes=64)
            nc.vector.quantize_mx(out=(c_ if (e, g) in TOK_QC else c_[:]).bitcast(FP8X4), scales=s_[:], in_=w1g[(e, g)][:])
            w1c[(e, g)], w1s[(e, g)] = c_, s_

        def copy_w2(e, eng):
            if W2_MERGE and e == 7:
                grp2 = w2pairs[0]
            elif e in W2_S:
                grp2 = keep.tile([P, (2 if W2_MERGE else 1) * G * N * PACK], BF16, tag="stk%d%d" % W2_S[e], name="w2g_k", align_bytes=256)
            else:
                grp2 = work3.tile([P, G * N * PACK], BF16, name="w2g", align_bytes=64)
            half = grp2[:]
            if W2_MERGE and e == 6:
                w2pairs.append(grp2)
                half = grp2[:, 0 : G * N * PACK]
            elif W2_MERGE and e == 7:
                half = grp2[:, G * N * PACK : 2 * G * N * PACK]
            dst = half.rearrange("p (g c i j) -> p g c j i", g=G, i=4, j=PACK)
            src = w2r[e][:].rearrange("p g j (c i) -> p g c j i", i=4)
            if eng == "S":
                nc.scalar.copy(out=dst, in_=src)
            else:
                nc.vector.tensor_copy(out=dst, in_=src)
            w2g[e] = grp2
            issue()

        def quant_w2_pair():
            c_ = work3.tile([P, 2 * G * N], U32, name="w2cp", bufs=1, align_bytes=64)
            s_ = work3.tile([P, 2 * G * N], U8, name="w2sp", bufs=1, align_bytes=64)
            nc.vector.quantize_mx(out=c_[:].bitcast(FP8X4), scales=s_[:], in_=w2pairs[0][:])
            for k in range(2):
                w2c[6 + k] = c_[:, k * G * N : (k + 1) * G * N]
                w2s[6 + k] = s_[:, k * G * N : (k + 1) * G * N]

        def quant_w2(e):
            c_ = work3.tile([P, G * N], U32, name="w2c", align_bytes=64)
            s_ = work3.tile([P, G * N], U8, name="w2s", align_bytes=64)
            nc.vector.quantize_mx(out=c_[:].bitcast(FP8X4), scales=s_[:], in_=w2g[e][:])
            w2c[e], w2s[e] = c_, s_

        def mm1(e, g):
            slots = slice(e * C, (e + 1) * C)
            p_ = psum_a.tile([P, PACK, C], F32, name="pa")
            for t in range(PACK):
                cols = slice(t * P, (t + 1) * P)
                nc.tensor.matmul_mx(
                    out=p_[:, t, :],
                    lhsT=w1c[(e, g)][:, cols].bitcast(FP8X4),
                    lhsT_scale=w1s[(e, g)][:, cols],
                    rhs=xc[:, slots].bitcast(FP8X4),
                    rhs_scale=xs[:, slots],
                    start=True,
                    stop=True,
                )
            pa[(e, g)] = p_

        def silu(e, g):
            if g == 0:
                if e in HB_S:
                    hb[e] = keep.tile([P, G * C * PACK], BF16, tag="tk%d%d" % HB_S[e], name="hb_k", align_bytes=256)
                elif e in TOK_HB:
                    hb[e] = token(TOK_HB[e], G * C * PACK, BF16, "hb_s")
                else:
                    hb[e] = work3.tile([P, G * C * PACK], BF16, name="hb", align_bytes=64)
                if e not in TOK_HC:
                    hc[e] = work3.tile([P, G * C], U32, name="hc", align_bytes=64)
                hs[e] = work3.tile([P, G * C], U8, name="hs", align_bytes=64)
            dst = hb[e][:, g * C * PACK : (g + 1) * C * PACK].rearrange("p (s t) -> p s t", t=PACK)
            src = pa[(e, g)][:].rearrange("p t s -> p s t")
            if (e, g) in SILU_TOK:
                nc.scalar.activation(dst, src, SILU, scale=stk[(e, g)][:])
            else:
                nc.scalar.activation(dst, src, SILU)

        def quant_h(e, gs):
            if e not in hc:
                hc[e] = token(TOK_HC[e], G * C, U32, "hc_s")
            a, b = gs[0], gs[-1] + 1
            nc.vector.quantize_mx(
                out=hc[e][:, a * C : b * C].bitcast(FP8X4),
                scales=hs[e][:, a * C : b * C],
                in_=hb[e][:, a * C * PACK : b * C * PACK],
            )

        def mm2(e):
            if e >= 6 and LASTSPLIT:
                py[("last", e)] = psum_y.tile([P, C], F32, name="pyl", bufs=1, tag="pyl%d" % e)
                bank = py[("last", e)][:]
            else:
                if e % 2 == 0:
                    py[e // 2] = psum_y.tile([P, PAIR], F32, name="py")
                bank = py[e // 2][:, (e % 2) * C : (e % 2 + 1) * C]
            for g in range(G):
                cols = slice(g * P, (g + 1) * P)
                nc.tensor.matmul_mx(
                    out=bank,
                    lhsT=w2c[e][:, cols].bitcast(FP8X4),
                    lhsT_scale=w2s[e][:, cols],
                    rhs=hc[e][:, cols].bitcast(FP8X4),
                    rhs_scale=hs[e][:, cols],
                    start=(g == 0),
                    stop=(g == G - 1),
                )

        def ycopy(q, slot):
            if slot is None:
                ysb[q] = keep.tile([P, PAIR], F32, name="ysb")[:]
                if LASTENG == "S":
                    nc.scalar.copy(out=ysb[q], in_=py[q][:])
                else:
                    nc.vector.tensor_copy(out=ysb[q], in_=py[q][:])
            else:
                ysb[q] = token(slot, PAIR, F32, "ysb_s")[:]
                nc.scalar.copy(out=ysb[q], in_=py[q][:])

        def scatter(q):
            nc.vector.tensor_tensor(
                win[:].indirect(offs_t[:, q * (PAIR // 16) : (q + 1) * (PAIR // 16)]),
                ysb[q],
                gate_t[q],
                MULT,
            )

        issue()

        for u in range(2):
            cast_x(u, 0, XV, "V")
            cast_x(u, XV, T, "S")
            gather_x(u)
            free(("x", u))
        nc.vector.quantize_mx(out=xc[:].bitcast(FP8X4), scales=xs[:], in_=xg[:])


        def rawkey(e, g):
            return ("w1", e) if ("w1", e) in LOADS else ("w1h", e, g)

        def free_piece(e, g):
            k = rawkey(e, g)
            if k[0] == "w1" and g == 0:
                return
            free(k)

        def layer2(e):
            quant_w2(e)
            mm2(e)

        def stage(s, e):
            if s == "c0":
                copy_w1(e, 0, SHARE[2 * e])
                if e < 7:
                    free_piece(e, 0)
            elif s == "c1":
                copy_w1(e, 1, SHARE[2 * e + 1])
            elif s == "y_":
                if e in Y_STAGE:
                    ycopy(Y_STAGE.index(e), rawkey(e, Y_PIECE))
            elif s == "sc":
                if e in Y_STAGE:
                    scatter(Y_STAGE.index(e))
            elif s == "fr":
                free_piece(e, 1)
            elif s == "wc":
                copy_w2(e, W2ENG[e])
            elif s == "q0":
                quant_w1(e, 0)
                mm1(e, 0)
            elif s == "q1":
                quant_w1(e, 1)
                mm1(e, 1)
            elif s == "wq":
                if not (W2_MERGE and e >= 6):
                    quant_w2(e)
                elif e == 7:
                    quant_w2_pair()
            elif s == "s0":
                silu(e, 0)
                if e in HALF_HQ:
                    quant_h(e, (0,))
            elif s == "s1":
                silu(e, 1)
                if e in HALF_HQ:
                    quant_h(e, (1,))
            elif s == "hq":
                if e not in HALF_HQ:
                    quant_h(e, (0, 1))
            elif s == "m2":
                if not (W2_MERGE and e == 6):
                    mm2(e - 1) if W2_MERGE and e == 7 else None
                    mm2(e)

        for step in range(E + 2):
            for s in (LAST_ORDER if step >= LAST_FROM else ORDER):
                e = step - int(s[2:])
                if 0 <= e < E:
                    stage(s[:2], e)
        if LASTSPLIT:
            ysb[3] = keep.tile([P, PAIR], F32, name="ysb")[:]
            nc.scalar.copy(out=ysb[3][:, 0:C], in_=py[("last", 6)][:])
            if LASTENG == "S":
                nc.scalar.copy(out=ysb[3][:, C:PAIR], in_=py[("last", 7)][:])
            else:
                nc.vector.tensor_copy(out=ysb[3][:, C:PAIR], in_=py[("last", 7)][:])
        else:
            ycopy(3, None)
        scatter(3)

        nc.sync.dma_start(out=out, in_=win[:])
